import numpy as np, ml_dtypes
CORES = [34,162,290,418,42,426]
N = 6
C = 256
def setup_inputs(rng):
    x = 150 * rng.standard_normal((1, 128, C), dtype=np.float32) + 2 * rng.standard_normal((N, 128, C), dtype=np.float32)
    x = (x + rng.uniform(100, 300, (1, 128, C)) * (rng.random((1, 128, C)) < 0.7) * (rng.random((N, 128, C)) < 0.5)).astype(np.float32)
    return {"x": x}
def setup_inputs_trail(rng):
    d = setup_inputs(rng); x = d["x"].copy(); t = int(rng.integers(N))
    x[t] = np.delete(x, t, axis=0).max(axis=0) - rng.uniform(3.0, 20.0, x[t].shape).astype(np.float32)
    return {"x": x}
def reference(x):
    X = x.astype(np.float64)
    P = np.exp(X - X.max(axis=0))
    return {"y": (P / P.sum(axis=0)).astype(ml_dtypes.bfloat16)}

@@ -1,0 +1,139 @@
+from concourse.mybir import AluOpType, ActivationFunctionType
+
+C = 256
+HALVES = ((0, C // 2), (C // 2, C))
+
+SQ_SCALE = 0.9778153589291791
+SQ_BIAS = 0.45741611243474367
+GAMMA = -0.20580551923485052
+
+SCRATCH = {
+    "xs": ("sbuf", [128, C], "float32"),
+    "xb": ("sbuf", [128, C], "float32"),
+    "xc": ("sbuf", [128, C], "float32"),
+    "la": ("sbuf", [128, C], "float32"),
+    "lb": ("sbuf", [128, C], "float32"),
+    "d1": ("sbuf", [128, C], "float32"),
+    "d2": ("sbuf", [128, C], "float32"),
+    "d3": ("sbuf", [128, C], "float32"),
+    "t1": ("sbuf", [128, C], "float32"),
+    "t2": ("sbuf", [128, C], "float32"),
+    "yb": ("sbuf", [128, C], "bfloat16"),
+    "ap": ("psum", [128, C], "float32"),
+    "m1": ("psum", [128, C], "float32"),
+    "l1": ("psum", [128, C], "float32"),
+    "m2": ("psum", [128, C], "float32"),
+    "lp": ("psum", [128, C], "float32"),
+    "w": ("psum", [128, C], "float32"),
+}
+N_CSEM = 40
+SEMAPHORES = ["loaded", "arr1", "arr2", "arr3", "sent", "stored"] + ["c%d" % i for i in range(N_CSEM)]
+
+
+def rank_program(g, core, T, topo):
+    if T.rank_of(core) is None:
+        return
+    V, S, Y = g.vector, g.scalar, g.sync
+    A, F = AluOpType, ActivationFunctionType
+    sem = T.sem
+
+    my_rack = topo.rack(topo.host(core))
+    ring = [c for c in T.cores if topo.rack(topo.host(c)) == my_rack]
+    i = ring.index(core)
+    nxt, prv = ring[(i + 1) % len(ring)], ring[(i - 1) % len(ring)]
+    partner = [c for c in T.cores if topo.rack(topo.host(c)) != my_rack
+               and topo.chip(c) == topo.chip(core) and topo.may_write(core, c)][0]
+
+    used = [0]
+
+    def new():
+        used[0] += 1
+        return sem["c%d" % (used[0] - 1)]
+
+    def engines(mask):
+        return bin(mask).count("1")
+
+    sent = [0]
+
+    def send(dst, out_ap, in_ap, rsem):
+        rid, pid = topo.addr(dst, core)
+        mask = topo.mask(core, dst)
+        g.remote_dma(out_ap, in_ap, rsem, sem.sent, pid, rid, mask)
+        sent[0] += engines(mask)
+
+    n1, n2, n3 = (engines(topo.mask(s, core)) for s in (prv, nxt, partner))
+
+    Y.dma_start(T.xs[:], T.x[:]).then_inc(sem.loaded, 16)
+
+    g.wait_ge(sem.loaded, 16)
+    send(nxt, T.xb[:], T.xs[:], sem.arr1)
+    send(prv, T.xc[:], T.xs[:], sem.arr2)
+
+    def merge(acc, other, d, t, m, outs):
+        s_d = [new(), new()]
+        for h, (a, b) in enumerate(HALVES):
+            V.tensor_tensor(d[:, a:b], acc[:, a:b], other[:, a:b], A.subtract).then_inc(s_d[h], 1)
+        s_prev = s_d
+        for func, kw in ((F.Abs, {}), (F.Sigmoid, {"scale": -1.0}), (F.Square, {"scale": SQ_SCALE, "bias": SQ_BIAS})):
+            s_now = [new(), new()]
+            for h, (a, b) in enumerate(HALVES):
+                S.wait_ge(s_prev[h], 1)
+                src = d if func == F.Abs else t
+                S.activation(t[:, a:b], src[:, a:b], func, **kw).then_inc(s_now[h], 1)
+            s_prev = s_now
+        s_m, s_mg = new(), new()
+        V.tensor_tensor(m[:], acc[:], other[:], A.max).then_inc(s_m, 1)
+        V.wait_ge(s_m, 1)
+        V.tensor_scalar(m[:], m[:], GAMMA, None, A.add).then_inc(s_mg, 1)
+        V.wait_ge(s_mg, 1)
+        res = []
+        for k, out in enumerate(outs):
+            s_o = [new(), new()]
+            for h, (a, b) in enumerate(HALVES):
+                if k == 0:
+                    V.wait_ge(s_prev[h], 1)
+                V.tensor_tensor(out[:, a:b], m[:, a:b], t[:, a:b], A.add).then_inc(s_o[h], 1)
+            res.append(s_o)
+        return res
+
+    s_ap = new()
+    V.wait_ge(sem.loaded, 16)
+    V.tensor_copy(T.ap[:], T.xs[:]).then_inc(s_ap, 1)
+    V.wait_ge(s_ap, 1)
+    V.wait_ge(sem.arr1, n1)
+    (s_l1,) = merge(T.ap, T.xb, T.d1, T.t1, T.m1, [T.l1])
+
+    V.wait_ge(sem.arr2, n2)
+    for s in s_l1:
+        V.wait_ge(s, 1)
+    s_la, s_lp = merge(T.l1, T.xc, T.d2, T.t2, T.m2, [T.la, T.lp])
+
+    for s in s_la:
+        g.wait_ge(s, 1)
+    send(partner, T.lb[:], T.la[:], sem.arr3)
+
+    s_pp, s_w = new(), new()
+    S.activation(T.d1[:], T.d1[:], F.Sigmoid).then_inc(s_pp, 1)
+    S.activation(T.d2[:], T.d2[:], F.Sigmoid).then_inc(s_pp, 1)
+    V.wait_ge(s_pp, 2)
+    V.tensor_tensor(T.w[:], T.d1[:], T.d2[:], A.mult).then_inc(s_w, 1)
+
+    for s in s_lp:
+        V.wait_ge(s, 1)
+    V.wait_ge(sem.arr3, n3)
+    s_d3, s_p3, s_y = [new(), new()], [new(), new()], new()
+    for h, (a, b) in enumerate(HALVES):
+        V.tensor_tensor(T.d3[:, a:b], T.lp[:, a:b], T.lb[:, a:b], A.subtract).then_inc(s_d3[h], 1)
+    for h, (a, b) in enumerate(HALVES):
+        S.wait_ge(s_d3[h], 1)
+        S.activation(T.d3[:, a:b], T.d3[:, a:b], F.Sigmoid).then_inc(s_p3[h], 1)
+    V.wait_ge(s_w, 1)
+    for h, (a, b) in enumerate(HALVES):
+        V.wait_ge(s_p3[h], 1)
+        V.tensor_tensor(T.yb[:, a:b], T.w[:, a:b], T.d3[:, a:b], A.mult).then_inc(s_y, 1)
+
+    Y.wait_ge(s_y, len(HALVES))
+    Y.dma_start(T.y[:], T.yb[:]).then_inc(sem.stored, 16)
+    Y.wait_ge(sem.stored, 16)
+
+    g.wait_ge(sem.sent, sent[0])

@@ -1,33 +1,21 @@
+from concourse.bass import DstId, RemoteDMATransfer
 from concourse.mybir import AluOpType, ActivationFunctionType
 
 C = 256
-HALVES = ((0, C // 2), (C // 2, C))
+H = C // 2
 
 SQ_SCALE = 0.9778153589291791
 SQ_BIAS = 0.45741611243474367
 GAMMA = -0.20580551923485052
 
-SCRATCH = {
-    "xs": ("sbuf", [128, C], "float32"),
-    "xb": ("sbuf", [128, C], "float32"),
-    "xc": ("sbuf", [128, C], "float32"),
-    "la": ("sbuf", [128, C], "float32"),
-    "lb": ("sbuf", [128, C], "float32"),
-    "d1": ("sbuf", [128, C], "float32"),
-    "d2": ("sbuf", [128, C], "float32"),
-    "d3": ("sbuf", [128, C], "float32"),
-    "t1": ("sbuf", [128, C], "float32"),
-    "t2": ("sbuf", [128, C], "float32"),
-    "yb": ("sbuf", [128, C], "bfloat16"),
-    "ap": ("psum", [128, C], "float32"),
-    "m1": ("psum", [128, C], "float32"),
-    "l1": ("psum", [128, C], "float32"),
-    "m2": ("psum", [128, C], "float32"),
-    "lp": ("psum", [128, C], "float32"),
-    "w": ("psum", [128, C], "float32"),
-}
-N_CSEM = 40
-SEMAPHORES = ["loaded", "arr1", "arr2", "arr3", "sent", "stored"] + ["c%d" % i for i in range(N_CSEM)]
+SCRATCH = {"xs": ("sbuf", [128, C], "float32"), "yb": ("sbuf", [128, C], "bfloat16")}
+for _n in ("xb", "xc", "xq", "lb", "gv", "gn", "la", "gq", "dq", "d1", "d2", "d3", "d4", "d5", "tq", "t1", "t2", "t4"):
+    SCRATCH[_n] = ("sbuf", [128, H], "float32")
+PS_SLOTS = ("ap", "aq", "mq", "m1", "m2", "m4", "gp", "l1", "lp", "hp", "wp", "wq")
+for _k in range(len(PS_SLOTS) // 4):
+    SCRATCH["ps%d" % _k] = ("psum", [128, 4 * H], "float32")
+N_CSEM = 42
+SEMAPHORES = ["loaded", "arr1", "arr2", "arrq", "arr3", "arr4", "arr5", "sent", "stored"] + ["c%d" % i for i in range(N_CSEM)]
 
 
 def rank_program(g, core, T, topo):
@@ -37,6 +25,10 @@ def rank_program(g, core, T, topo):
     A, F = AluOpType, ActivationFunctionType
     sem = T.sem
 
+    def ps(name):
+        k = PS_SLOTS.index(name)
+        return T["ps%d" % (k // 4)][:, (k % 4) * H:(k % 4 + 1) * H]
+
     my_rack = topo.rack(topo.host(core))
     ring = [c for c in T.cores if topo.rack(topo.host(c)) == my_rack]
     i = ring.index(core)
@@ -44,96 +36,124 @@ def rank_program(g, core, T, topo):
     partner = [c for c in T.cores if topo.rack(topo.host(c)) != my_rack
                and topo.chip(c) == topo.chip(core) and topo.may_write(core, c)][0]
 
+    def deal(src, dst, k):
+        e = [j for j in range(16) if (topo.mask(src, dst) >> j) & 1]
+        return e[k::2]
+
+    def bits(e):
+        return sum(1 << j for j in e)
+
     used = [0]
 
     def new():
         used[0] += 1
         return sem["c%d" % (used[0] - 1)]
 
-    def engines(mask):
-        return bin(mask).count("1")
-
     sent = [0]
 
-    def send(dst, out_ap, in_ap, rsem):
-        rid, pid = topo.addr(dst, core)
-        mask = topo.mask(core, dst)
-        g.remote_dma(out_ap, in_ap, rsem, sem.sent, pid, rid, mask)
-        sent[0] += engines(mask)
+    def send(jobs):
+        tr = []
+        for dst, out_ap, in_ap, rsem, k in jobs:
+            rid, pid = topo.addr(dst, core)
+            e = deal(core, dst, k)
+            tr.append(RemoteDMATransfer(dst_ids=[DstId(rid=rid, pnc=pid)], dma_engine_mask=bits(e), remote_sem=rsem,
+                                        src=in_ap, dst=out_ap))
+            sent[0] += len(e)
+        g.remote_dma_fused(tr, local_sem=sem.sent)
 
-    n1, n2, n3 = (engines(topo.mask(s, core)) for s in (prv, nxt, partner))
+    RING, CABLE = 0, 1
+    n_prv, n_nxt, n_par = len(deal(prv, core, RING)), len(deal(nxt, core, RING)), len(deal(partner, core, CABLE))
 
     Y.dma_start(T.xs[:], T.x[:]).then_inc(sem.loaded, 16)
 
     g.wait_ge(sem.loaded, 16)
-    send(nxt, T.xb[:], T.xs[:], sem.arr1)
-    send(prv, T.xc[:], T.xs[:], sem.arr2)
+    send([(nxt, T.xb[:], T.xs[:, 0:H], sem.arr1, RING), (partner, T.xq[:], T.xs[:, H:C], sem.arrq, CABLE)])
+    send([(prv, T.xc[:], T.xs[:, 0:H], sem.arr2, RING)])
 
-    def merge(acc, other, d, t, m, outs):
-        s_d = [new(), new()]
-        for h, (a, b) in enumerate(HALVES):
-            V.tensor_tensor(d[:, a:b], acc[:, a:b], other[:, a:b], A.subtract).then_inc(s_d[h], 1)
-        s_prev = s_d
+    def merge_a(acc, other, d, t, m):
+        s = new()
+        V.tensor_tensor(d, acc, other, A.subtract).then_inc(s, 1)
+        src = d
         for func, kw in ((F.Abs, {}), (F.Sigmoid, {"scale": -1.0}), (F.Square, {"scale": SQ_SCALE, "bias": SQ_BIAS})):
-            s_now = [new(), new()]
-            for h, (a, b) in enumerate(HALVES):
-                S.wait_ge(s_prev[h], 1)
-                src = d if func == F.Abs else t
-                S.activation(t[:, a:b], src[:, a:b], func, **kw).then_inc(s_now[h], 1)
-            s_prev = s_now
+            S.wait_ge(s, 1)
+            s = new()
+            S.activation(t, src, func, **kw).then_inc(s, 1)
+            src = t
         s_m, s_mg = new(), new()
-        V.tensor_tensor(m[:], acc[:], other[:], A.max).then_inc(s_m, 1)
+        V.tensor_tensor(m, acc, other, A.max).then_inc(s_m, 1)
         V.wait_ge(s_m, 1)
-        V.tensor_scalar(m[:], m[:], GAMMA, None, A.add).then_inc(s_mg, 1)
-        V.wait_ge(s_mg, 1)
+        V.tensor_scalar(m, m, GAMMA, None, A.add).then_inc(s_mg, 1)
+        return s, s_mg
+
+    def merge_b(st, t, m, outs):
+        V.wait_ge(st[1], 1)
+        V.wait_ge(st[0], 1)
         res = []
-        for k, out in enumerate(outs):
-            s_o = [new(), new()]
-            for h, (a, b) in enumerate(HALVES):
-                if k == 0:
-                    V.wait_ge(s_prev[h], 1)
-                V.tensor_tensor(out[:, a:b], m[:, a:b], t[:, a:b], A.add).then_inc(s_o[h], 1)
-            res.append(s_o)
+        for out in outs:
+            res.append(new())
+            V.tensor_tensor(out, m, t, A.add).then_inc(res[-1], 1)
         return res
 
     s_ap = new()
     V.wait_ge(sem.loaded, 16)
-    V.tensor_copy(T.ap[:], T.xs[:]).then_inc(s_ap, 1)
+    V.tensor_copy(T.ps0[:, 0:C], T.xs[:]).then_inc(s_ap, 1)
     V.wait_ge(s_ap, 1)
-    V.wait_ge(sem.arr1, n1)
-    (s_l1,) = merge(T.ap, T.xb, T.d1, T.t1, T.m1, [T.l1])
+    V.wait_ge(sem.arrq, n_par)
+    st_q = merge_a(ps("aq"), T.xq[:], T.dq[:], T.tq[:], ps("mq"))
+    V.wait_ge(sem.arr1, n_prv)
+    st_1 = merge_a(ps("ap"), T.xb[:], T.d1[:], T.t1[:], ps("m1"))
+    s_gq, s_gp = merge_b(st_q, T.tq[:], ps("mq"), [T.gq[:], ps("gp")])
+    (s_l1,) = merge_b(st_1, T.t1[:], ps("m1"), [ps("l1")])
+    V.wait_ge(s_l1, 1)
+    V.wait_ge(sem.arr2, n_nxt)
+    st_2 = merge_a(ps("l1"), T.xc[:], T.d2[:], T.t2[:], ps("m2"))
+    s_la, s_lp = merge_b(st_2, T.t2[:], ps("m2"), [T.la[:], ps("lp")])
 
-    V.wait_ge(sem.arr2, n2)
-    for s in s_l1:
-        V.wait_ge(s, 1)
-    s_la, s_lp = merge(T.l1, T.xc, T.d2, T.t2, T.m2, [T.la, T.lp])
+    g.wait_ge(s_gq, 1)
+    send([(nxt, T.gv[:], T.gq[:], sem.arr4, RING)])
+    send([(prv, T.gn[:], T.gq[:], sem.arr5, RING)])
+    g.wait_ge(s_la, 1)
+    send([(partner, T.lb[:], T.la[:], sem.arr3, CABLE)])
 
-    for s in s_la:
-        g.wait_ge(s, 1)
-    send(partner, T.lb[:], T.la[:], sem.arr3)
-
-    s_pp, s_w = new(), new()
+    s_sq, s_pp, s_wp = new(), new(), new()
+    S.activation(T.dq[:], T.dq[:], F.Sigmoid).then_inc(s_sq, 1)
     S.activation(T.d1[:], T.d1[:], F.Sigmoid).then_inc(s_pp, 1)
     S.activation(T.d2[:], T.d2[:], F.Sigmoid).then_inc(s_pp, 1)
     V.wait_ge(s_pp, 2)
-    V.tensor_tensor(T.w[:], T.d1[:], T.d2[:], A.mult).then_inc(s_w, 1)
+    V.tensor_tensor(ps("wp"), T.d1[:], T.d2[:], A.mult).then_inc(s_wp, 1)
 
-    for s in s_lp:
-        V.wait_ge(s, 1)
-    V.wait_ge(sem.arr3, n3)
-    s_d3, s_p3, s_y = [new(), new()], [new(), new()], new()
-    for h, (a, b) in enumerate(HALVES):
-        V.tensor_tensor(T.d3[:, a:b], T.lp[:, a:b], T.lb[:, a:b], A.subtract).then_inc(s_d3[h], 1)
-    for h, (a, b) in enumerate(HALVES):
-        S.wait_ge(s_d3[h], 1)
-        S.activation(T.d3[:, a:b], T.d3[:, a:b], F.Sigmoid).then_inc(s_p3[h], 1)
-    V.wait_ge(s_w, 1)
-    for h, (a, b) in enumerate(HALVES):
-        V.wait_ge(s_p3[h], 1)
-        V.tensor_tensor(T.yb[:, a:b], T.w[:, a:b], T.d3[:, a:b], A.mult).then_inc(s_y, 1)
+    V.wait_ge(s_gp, 1)
+    V.wait_ge(sem.arr4, n_prv)
+    st_4 = merge_a(ps("gp"), T.gv[:], T.d4[:], T.t4[:], ps("m4"))
+    (s_hp,) = merge_b(st_4, T.t4[:], ps("m4"), [ps("hp")])
+    s_s4, s_wq = new(), new()
+    S.activation(T.d4[:], T.d4[:], F.Sigmoid).then_inc(s_s4, 1)
+    V.wait_ge(s_sq, 1)
+    V.wait_ge(s_s4, 1)
+    V.tensor_tensor(ps("wq"), T.dq[:], T.d4[:], A.mult).then_inc(s_wq, 1)
 
-    Y.wait_ge(s_y, len(HALVES))
-    Y.dma_start(T.y[:], T.yb[:]).then_inc(sem.stored, 16)
-    Y.wait_ge(sem.stored, 16)
+    s_d3, s_d5, s_p3, s_p5, s_yp, s_yq = new(), new(), new(), new(), new(), new()
+    V.wait_ge(s_lp, 1)
+    V.wait_ge(sem.arr3, n_par)
+    V.tensor_tensor(T.d3[:], ps("lp"), T.lb[:], A.subtract).then_inc(s_d3, 1)
+    V.wait_ge(s_hp, 1)
+    V.wait_ge(sem.arr5, n_nxt)
+    V.tensor_tensor(T.d5[:], ps("hp"), T.gn[:], A.subtract).then_inc(s_d5, 1)
+    S.wait_ge(s_d3, 1)
+    S.activation(T.d3[:], T.d3[:], F.Sigmoid).then_inc(s_p3, 1)
+    S.wait_ge(s_d5, 1)
+    S.activation(T.d5[:], T.d5[:], F.Sigmoid).then_inc(s_p5, 1)
+    V.wait_ge(s_wp, 1)
+    V.wait_ge(s_p3, 1)
+    V.tensor_tensor(T.yb[:, 0:H], ps("wp"), T.d3[:], A.mult).then_inc(s_yp, 1)
+    V.wait_ge(s_wq, 1)
+    V.wait_ge(s_p5, 1)
+    V.tensor_tensor(T.yb[:, H:C], ps("wq"), T.d5[:], A.mult).then_inc(s_yq, 1)
+
+    Y.wait_ge(s_yp, 1)
+    Y.dma_start(T.y[:, 0:H], T.yb[:, 0:H]).then_inc(sem.stored, 16)
+    Y.wait_ge(s_yq, 1)
+    Y.dma_start(T.y[:, H:C], T.yb[:, H:C]).then_inc(sem.stored, 16)
+    Y.wait_ge(sem.stored, 32)
 
     g.wait_ge(sem.sent, sent[0])

@@ -1,20 +1,27 @@
-from concourse.bass import DstId, RemoteDMATransfer
 from concourse.mybir import AluOpType, ActivationFunctionType
 
 C = 256
-H = C // 2
+HP = 104
+HQ = C - HP
 
+R_T0 = 5.69
+R_SCALE = 0.15951068197070614
+R_GAMMA = 0.007537815109826294
 SQ_SCALE = 0.9778153589291791
 SQ_BIAS = 0.45741611243474367
 GAMMA = -0.20580551923485052
 
-SCRATCH = {"xs": ("sbuf", [128, C], "float32"), "yb": ("sbuf", [128, C], "bfloat16")}
-for _n in ("xb", "xc", "xq", "lb", "gv", "gn", "la", "gq", "dq", "d1", "d2", "d3", "d4", "d5", "tq", "t1", "t2", "t4"):
-    SCRATCH[_n] = ("sbuf", [128, H], "float32")
-PS_SLOTS = ("ap", "aq", "mq", "m1", "m2", "m4", "gp", "l1", "lp", "hp", "wp", "wq")
-for _k in range(len(PS_SLOTS) // 4):
-    SCRATCH["ps%d" % _k] = ("psum", [128, 4 * H], "float32")
-N_CSEM = 42
+SCRATCH = {"xs": ("sbuf", [128, C], "float32"), "yb": ("sbuf", [128, C], "bfloat16"), "px": ("psum", [128, C], "float32")}
+for _n in ("xb", "xc", "lb", "la", "d1", "d2", "d3", "t1", "t2"):
+    SCRATCH[_n] = ("sbuf", [128, HP], "float32")
+for _n in ("xq", "gv", "gn", "gq", "dq", "d4", "d5", "tq", "t4"):
+    SCRATCH[_n] = ("sbuf", [128, HQ], "float32")
+PS_P = ("m1", "m2", "l1", "lp", "wp")
+PS_Q = ("mq", "m4", "gp", "hp", "wq")
+PS_W = max(HP, HQ)
+for _k in range((len(PS_P + PS_Q) + 2) // 3):
+    SCRATCH["ps%d" % _k] = ("psum", [128, 3 * PS_W], "float32")
+N_CSEM = 45
 SEMAPHORES = ["loaded", "arr1", "arr2", "arrq", "arr3", "arr4", "arr5", "sent", "stored"] + ["c%d" % i for i in range(N_CSEM)]
 
 
@@ -26,8 +33,9 @@ def rank_program(g, core, T, topo):
     sem = T.sem
 
     def ps(name):
-        k = PS_SLOTS.index(name)
-        return T["ps%d" % (k // 4)][:, (k % 4) * H:(k % 4 + 1) * H]
+        k = (PS_P + PS_Q).index(name)
+        w = HP if name in PS_P else HQ
+        return T["ps%d" % (k // 3)][:, (k % 3) * PS_W:(k % 3) * PS_W + w]
 
     my_rack = topo.rack(topo.host(core))
     ring = [c for c in T.cores if topo.rack(topo.host(c)) == my_rack]
@@ -40,9 +48,6 @@ def rank_program(g, core, T, topo):
         e = [j for j in range(16) if (topo.mask(src, dst) >> j) & 1]
         return e[k::2]
 
-    def bits(e):
-        return sum(1 << j for j in e)
-
     used = [0]
 
     def new():
@@ -51,15 +56,11 @@ def rank_program(g, core, T, topo):
 
     sent = [0]
 
-    def send(jobs):
-        tr = []
-        for dst, out_ap, in_ap, rsem, k in jobs:
-            rid, pid = topo.addr(dst, core)
-            e = deal(core, dst, k)
-            tr.append(RemoteDMATransfer(dst_ids=[DstId(rid=rid, pnc=pid)], dma_engine_mask=bits(e), remote_sem=rsem,
-                                        src=in_ap, dst=out_ap))
-            sent[0] += len(e)
-        g.remote_dma_fused(tr, local_sem=sem.sent)
+    def send(dst, out_ap, in_ap, rsem, k):
+        rid, pid = topo.addr(dst, core)
+        e = deal(core, dst, k)
+        g.remote_dma(out_ap, in_ap, rsem, sem.sent, pid, rid, sum(1 << j for j in e))
+        sent[0] += len(e)
 
     RING, CABLE = 0, 1
     n_prv, n_nxt, n_par = len(deal(prv, core, RING)), len(deal(nxt, core, RING)), len(deal(partner, core, CABLE))
@@ -67,14 +68,19 @@ def rank_program(g, core, T, topo):
     Y.dma_start(T.xs[:], T.x[:]).then_inc(sem.loaded, 16)
 
     g.wait_ge(sem.loaded, 16)
-    send([(nxt, T.xb[:], T.xs[:, 0:H], sem.arr1, RING), (partner, T.xq[:], T.xs[:, H:C], sem.arrq, CABLE)])
-    send([(prv, T.xc[:], T.xs[:, 0:H], sem.arr2, RING)])
+    send(nxt, T.xb[:], T.xs[:, 0:HP], sem.arr1, RING)
+    send(partner, T.xq[:], T.xs[:, HP:C], sem.arrq, CABLE)
+    send(prv, T.xc[:], T.xs[:, 0:HP], sem.arr2, RING)
 
-    def merge_a(acc, other, d, t, m):
+    NO_TABLE = (((F.Abs, {}), (F.Relu, {"scale": -1.0, "bias": R_T0}), (F.Square, {"scale": R_SCALE}), (F.Square, {})),
+                R_GAMMA)
+    WITH_TABLE = (((F.Abs, {}), (F.Sigmoid, {"scale": -1.0}), (F.Square, {"scale": SQ_SCALE, "bias": SQ_BIAS})), GAMMA)
+
+    def merge_a(acc, other, d, t, m, way):
         s = new()
         V.tensor_tensor(d, acc, other, A.subtract).then_inc(s, 1)
         src = d
-        for func, kw in ((F.Abs, {}), (F.Sigmoid, {"scale": -1.0}), (F.Square, {"scale": SQ_SCALE, "bias": SQ_BIAS})):
+        for func, kw in way[0]:
             S.wait_ge(s, 1)
             s = new()
             S.activation(t, src, func, **kw).then_inc(s, 1)
@@ -82,7 +88,7 @@ def rank_program(g, core, T, topo):
         s_m, s_mg = new(), new()
         V.tensor_tensor(m, acc, other, A.max).then_inc(s_m, 1)
         V.wait_ge(s_m, 1)
-        V.tensor_scalar(m, m, GAMMA, None, A.add).then_inc(s_mg, 1)
+        V.tensor_scalar(m, m, way[1], None, A.add).then_inc(s_mg, 1)
         return s, s_mg
 
     def merge_b(st, t, m, outs):
@@ -96,35 +102,35 @@ def rank_program(g, core, T, topo):
 
     s_ap = new()
     V.wait_ge(sem.loaded, 16)
-    V.tensor_copy(T.ps0[:, 0:C], T.xs[:]).then_inc(s_ap, 1)
+    V.tensor_copy(T.px[:], T.xs[:]).then_inc(s_ap, 1)
     V.wait_ge(s_ap, 1)
-    V.wait_ge(sem.arrq, n_par)
-    st_q = merge_a(ps("aq"), T.xq[:], T.dq[:], T.tq[:], ps("mq"))
     V.wait_ge(sem.arr1, n_prv)
-    st_1 = merge_a(ps("ap"), T.xb[:], T.d1[:], T.t1[:], ps("m1"))
-    s_gq, s_gp = merge_b(st_q, T.tq[:], ps("mq"), [T.gq[:], ps("gp")])
+    st_1 = merge_a(T.px[:, 0:HP], T.xb[:], T.d1[:], T.t1[:], ps("m1"), NO_TABLE)
+    V.wait_ge(sem.arrq, n_par)
+    st_q = merge_a(T.px[:, HP:C], T.xq[:], T.dq[:], T.tq[:], ps("mq"), NO_TABLE)
     (s_l1,) = merge_b(st_1, T.t1[:], ps("m1"), [ps("l1")])
+    s_gq, s_gp = merge_b(st_q, T.tq[:], ps("mq"), [T.gq[:], ps("gp")])
     V.wait_ge(s_l1, 1)
     V.wait_ge(sem.arr2, n_nxt)
-    st_2 = merge_a(ps("l1"), T.xc[:], T.d2[:], T.t2[:], ps("m2"))
+    st_2 = merge_a(ps("l1"), T.xc[:], T.d2[:], T.t2[:], ps("m2"), NO_TABLE)
     s_la, s_lp = merge_b(st_2, T.t2[:], ps("m2"), [T.la[:], ps("lp")])
 
     g.wait_ge(s_gq, 1)
-    send([(nxt, T.gv[:], T.gq[:], sem.arr4, RING)])
-    send([(prv, T.gn[:], T.gq[:], sem.arr5, RING)])
+    send(nxt, T.gv[:], T.gq[:], sem.arr4, RING)
+    send(prv, T.gn[:], T.gq[:], sem.arr5, RING)
     g.wait_ge(s_la, 1)
-    send([(partner, T.lb[:], T.la[:], sem.arr3, CABLE)])
+    send(partner, T.lb[:], T.la[:], sem.arr3, CABLE)
 
     s_sq, s_pp, s_wp = new(), new(), new()
-    S.activation(T.dq[:], T.dq[:], F.Sigmoid).then_inc(s_sq, 1)
     S.activation(T.d1[:], T.d1[:], F.Sigmoid).then_inc(s_pp, 1)
     S.activation(T.d2[:], T.d2[:], F.Sigmoid).then_inc(s_pp, 1)
+    S.activation(T.dq[:], T.dq[:], F.Sigmoid).then_inc(s_sq, 1)
     V.wait_ge(s_pp, 2)
     V.tensor_tensor(ps("wp"), T.d1[:], T.d2[:], A.mult).then_inc(s_wp, 1)
 
     V.wait_ge(s_gp, 1)
     V.wait_ge(sem.arr4, n_prv)
-    st_4 = merge_a(ps("gp"), T.gv[:], T.d4[:], T.t4[:], ps("m4"))
+    st_4 = merge_a(ps("gp"), T.gv[:], T.d4[:], T.t4[:], ps("m4"), WITH_TABLE)
     (s_hp,) = merge_b(st_4, T.t4[:], ps("m4"), [ps("hp")])
     s_s4, s_wq = new(), new()
     S.activation(T.d4[:], T.d4[:], F.Sigmoid).then_inc(s_s4, 1)
@@ -145,15 +151,15 @@ def rank_program(g, core, T, topo):
     S.activation(T.d5[:], T.d5[:], F.Sigmoid).then_inc(s_p5, 1)
     V.wait_ge(s_wp, 1)
     V.wait_ge(s_p3, 1)
-    V.tensor_tensor(T.yb[:, 0:H], ps("wp"), T.d3[:], A.mult).then_inc(s_yp, 1)
+    V.tensor_tensor(T.yb[:, 0:HP], ps("wp"), T.d3[:], A.mult).then_inc(s_yp, 1)
     V.wait_ge(s_wq, 1)
     V.wait_ge(s_p5, 1)
-    V.tensor_tensor(T.yb[:, H:C], ps("wq"), T.d5[:], A.mult).then_inc(s_yq, 1)
+    V.tensor_tensor(T.yb[:, HP:C], ps("wq"), T.d5[:], A.mult).then_inc(s_yq, 1)
 
     Y.wait_ge(s_yp, 1)
-    Y.dma_start(T.y[:, 0:H], T.yb[:, 0:H]).then_inc(sem.stored, 16)
+    Y.dma_start(T.y[:, 0:HP], T.yb[:, 0:HP]).then_inc(sem.stored, 16)
     Y.wait_ge(s_yq, 1)
-    Y.dma_start(T.y[:, H:C], T.yb[:, H:C]).then_inc(sem.stored, 16)
+    Y.dma_start(T.y[:, HP:C], T.yb[:, HP:C]).then_inc(sem.stored, 16)
     Y.wait_ge(sem.stored, 32)
 
     g.wait_ge(sem.sent, sent[0])

@@ -1,8 +1,11 @@
 from concourse.mybir import AluOpType, ActivationFunctionType
 
+WORLD = 512
 C = 256
-HP = 104
-HQ = C - HP
+CB = 48
+CA = C - CB
+HP = 80
+HQ = CA - HP
 
 R_T0 = 5.69
 R_SCALE = 0.15951068197070614
@@ -11,37 +14,54 @@ SQ_SCALE = 0.9778153589291791
 SQ_BIAS = 0.45741611243474367
 GAMMA = -0.20580551923485052
 
-SCRATCH = {"xs": ("sbuf", [128, C], "float32"), "yb": ("sbuf", [128, C], "bfloat16"), "px": ("psum", [128, C], "float32")}
+SCRATCH = {"xs": ("sbuf", [128, C], "float32"), "yb": ("sbuf", [128, C], "bfloat16"), "px": ("psum", [128, CA], "float32")}
 for _n in ("xb", "xc", "lb", "la", "d1", "d2", "d3", "t1", "t2"):
     SCRATCH[_n] = ("sbuf", [128, HP], "float32")
 for _n in ("xq", "gv", "gn", "gq", "dq", "d4", "d5", "tq", "t4"):
     SCRATCH[_n] = ("sbuf", [128, HQ], "float32")
+for _n in ("xh", "hxq", "hgv", "hgn", "hgq", "hdq", "hd4", "hd5", "htq", "ht4"):
+    SCRATCH[_n] = ("sbuf", [128, CB], "float32")
+SCRATCH["yh"] = ("sbuf", [128, CB], "bfloat16")
 PS_P = ("m1", "m2", "l1", "lp", "wp")
 PS_Q = ("mq", "m4", "gp", "hp", "wq")
 PS_W = max(HP, HQ)
 for _k in range((len(PS_P + PS_Q) + 2) // 3):
     SCRATCH["ps%d" % _k] = ("psum", [128, 3 * PS_W], "float32")
+PS_B = ("px", "mq", "m4", "gp", "hp", "wq")
+SCRATCH["pb"] = ("psum", [128, len(PS_B) * CB], "float32")
 N_CSEM = 45
-SEMAPHORES = ["loaded", "arr1", "arr2", "arrq", "arr3", "arr4", "arr5", "sent", "stored"] + ["c%d" % i for i in range(N_CSEM)]
+SEMAPHORES = ["loaded", "loadb", "arr1", "arr2", "arrq", "arr3", "arr4", "arr5", "arrh", "arry", "sent", "stored",
+              "storedb"] + ["c%d" % i for i in range(N_CSEM)]
 
 
 def rank_program(g, core, T, topo):
-    if T.rank_of(core) is None:
+    def same_chip(a, b):
+        return topo.host(a) == topo.host(b) and topo.chip(a) == topo.chip(b)
+
+    if not [c for c in T.cores if same_chip(c, core)]:
         return
+
+    def helper_of(c):
+        return [k for k in range(WORLD) if same_chip(k, c) and topo.die(k) != topo.die(c) and T.rank_of(k) is None
+                and all(topo.may_write(k, d) for d in T.cores if d != c and topo.may_write(c, d))][0]
+
+    helpers = [helper_of(c) for c in T.cores]
+    if T.rank_of(core) is not None:
+        lane, is_rank = list(T.cores), True
+    elif core in helpers:
+        lane, is_rank = helpers, False
+    else:
+        return
+
     V, S, Y = g.vector, g.scalar, g.sync
     A, F = AluOpType, ActivationFunctionType
     sem = T.sem
 
-    def ps(name):
-        k = (PS_P + PS_Q).index(name)
-        w = HP if name in PS_P else HQ
-        return T["ps%d" % (k // 3)][:, (k % 3) * PS_W:(k % 3) * PS_W + w]
-
     my_rack = topo.rack(topo.host(core))
-    ring = [c for c in T.cores if topo.rack(topo.host(c)) == my_rack]
+    ring = [c for c in lane if topo.rack(topo.host(c)) == my_rack]
     i = ring.index(core)
     nxt, prv = ring[(i + 1) % len(ring)], ring[(i - 1) % len(ring)]
-    partner = [c for c in T.cores if topo.rack(topo.host(c)) != my_rack
+    partner = [c for c in lane if topo.rack(topo.host(c)) != my_rack
                and topo.chip(c) == topo.chip(core) and topo.may_write(core, c)][0]
 
     def deal(src, dst, k):
@@ -56,21 +76,12 @@ def rank_program(g, core, T, topo):
 
     sent = [0]
 
-    def send(dst, out_ap, in_ap, rsem, k):
+    def send(dst, out_ap, in_ap, rsem, e):
         rid, pid = topo.addr(dst, core)
-        e = deal(core, dst, k)
         g.remote_dma(out_ap, in_ap, rsem, sem.sent, pid, rid, sum(1 << j for j in e))
         sent[0] += len(e)
 
     RING, CABLE = 0, 1
-    n_prv, n_nxt, n_par = len(deal(prv, core, RING)), len(deal(nxt, core, RING)), len(deal(partner, core, CABLE))
-
-    Y.dma_start(T.xs[:], T.x[:]).then_inc(sem.loaded, 16)
-
-    g.wait_ge(sem.loaded, 16)
-    send(nxt, T.xb[:], T.xs[:, 0:HP], sem.arr1, RING)
-    send(partner, T.xq[:], T.xs[:, HP:C], sem.arrq, CABLE)
-    send(prv, T.xc[:], T.xs[:, 0:HP], sem.arr2, RING)
 
     NO_TABLE = (((F.Abs, {}), (F.Relu, {"scale": -1.0, "bias": R_T0}), (F.Square, {"scale": R_SCALE}), (F.Square, {})),
                 R_GAMMA)
@@ -100,14 +111,90 @@ def rank_program(g, core, T, topo):
             V.tensor_tensor(out, m, t, A.add).then_inc(res[-1], 1)
         return res
 
+    if not is_rank:
+        rank = T.cores[helpers.index(core)]
+
+        def pb(name):
+            k = PS_B.index(name)
+            return T.pb[:, k * CB:(k + 1) * CB]
+
+        r_ring = [c for c in T.cores if topo.rack(topo.host(c)) == my_rack]
+        n_in = len(deal(rank, r_ring[(r_ring.index(rank) + 1) % len(r_ring)], RING))
+        e_nxt, e_prv, e_par = deal(core, nxt, RING), deal(core, prv, RING), deal(core, partner, RING)
+        e_home = [j for j in e_nxt if (topo.mask(core, rank) >> j) & 1]
+        n_prv, n_nxt, n_par = len(deal(prv, core, RING)), len(deal(nxt, core, RING)), len(deal(partner, core, RING))
+
+        g.wait_ge(sem.arrh, n_in)
+        send(partner, T.hxq[:], T.xh[:], sem.arrq, e_par)
+
+        s_ap = new()
+        V.wait_ge(sem.arrh, n_in)
+        V.tensor_copy(pb("px"), T.xh[:]).then_inc(s_ap, 1)
+        V.wait_ge(s_ap, 1)
+        V.wait_ge(sem.arrq, n_par)
+        st_q = merge_a(pb("px"), T.hxq[:], T.hdq[:], T.htq[:], pb("mq"), NO_TABLE)
+        s_gq, s_gp = merge_b(st_q, T.htq[:], pb("mq"), [T.hgq[:], pb("gp")])
+
+        g.wait_ge(s_gq, 1)
+        send(nxt, T.hgv[:], T.hgq[:], sem.arr4, e_nxt)
+        send(prv, T.hgn[:], T.hgq[:], sem.arr5, e_prv)
+
+        s_sq = new()
+        S.activation(T.hdq[:], T.hdq[:], F.Sigmoid).then_inc(s_sq, 1)
+        V.wait_ge(s_gp, 1)
+        V.wait_ge(sem.arr4, n_prv)
+        st_4 = merge_a(pb("gp"), T.hgv[:], T.hd4[:], T.ht4[:], pb("m4"), WITH_TABLE)
+        (s_hp,) = merge_b(st_4, T.ht4[:], pb("m4"), [pb("hp")])
+        s_s4, s_wq, s_d5, s_p5, s_y = new(), new(), new(), new(), new()
+        S.activation(T.hd4[:], T.hd4[:], F.Sigmoid).then_inc(s_s4, 1)
+        V.wait_ge(s_sq, 1)
+        V.wait_ge(s_s4, 1)
+        V.tensor_tensor(pb("wq"), T.hdq[:], T.hd4[:], A.mult).then_inc(s_wq, 1)
+        V.wait_ge(s_hp, 1)
+        V.wait_ge(sem.arr5, n_nxt)
+        V.tensor_tensor(T.hd5[:], pb("hp"), T.hgn[:], A.subtract).then_inc(s_d5, 1)
+        S.wait_ge(s_d5, 1)
+        S.activation(T.hd5[:], T.hd5[:], F.Sigmoid).then_inc(s_p5, 1)
+        V.wait_ge(s_wq, 1)
+        V.wait_ge(s_p5, 1)
+        V.tensor_tensor(T.yh[:], pb("wq"), T.hd5[:], A.mult).then_inc(s_y, 1)
+
+        g.wait_ge(s_y, 1)
+        send(rank, T.yb[:, CA:C], T.yh[:], sem.arry, e_home)
+        g.wait_ge(sem.sent, sent[0])
+        return
+
+    helper = helpers[T.rank_of(core)]
+
+    def ps(name):
+        k = (PS_P + PS_Q).index(name)
+        w = HP if name in PS_P else HQ
+        return T["ps%d" % (k // 3)][:, (k % 3) * PS_W:(k % 3) * PS_W + w]
+
+    e_nxt, e_prv, e_par = deal(core, nxt, RING), deal(core, prv, RING), deal(core, partner, CABLE)
+    e_help = [j for j in e_nxt if (topo.mask(core, helper) >> j) & 1]
+    n_prv, n_nxt, n_par = len(deal(prv, core, RING)), len(deal(nxt, core, RING)), len(deal(partner, core, CABLE))
+    h_ring = [c for c in helpers if topo.rack(topo.host(c)) == my_rack]
+    n_home = len(deal(helper, h_ring[(h_ring.index(helper) + 1) % len(h_ring)], RING))
+
+    S.dma_start(T.xs[:, CA:C], T.x[:, CA:C]).then_inc(sem.loadb, 16)
+    Y.dma_start(T.xs[:, 0:CA], T.x[:, 0:CA]).then_inc(sem.loaded, 16)
+
+    g.wait_ge(sem.loadb, 16)
+    send(helper, T.xh[:], T.xs[:, CA:C], sem.arrh, e_help)
+    g.wait_ge(sem.loaded, 16)
+    send(nxt, T.xb[:], T.xs[:, 0:HP], sem.arr1, e_nxt)
+    send(partner, T.xq[:], T.xs[:, HP:CA], sem.arrq, e_par)
+    send(prv, T.xc[:], T.xs[:, 0:HP], sem.arr2, e_prv)
+
     s_ap = new()
     V.wait_ge(sem.loaded, 16)
-    V.tensor_copy(T.px[:], T.xs[:]).then_inc(s_ap, 1)
+    V.tensor_copy(T.px[:], T.xs[:, 0:CA]).then_inc(s_ap, 1)
     V.wait_ge(s_ap, 1)
     V.wait_ge(sem.arr1, n_prv)
     st_1 = merge_a(T.px[:, 0:HP], T.xb[:], T.d1[:], T.t1[:], ps("m1"), NO_TABLE)
     V.wait_ge(sem.arrq, n_par)
-    st_q = merge_a(T.px[:, HP:C], T.xq[:], T.dq[:], T.tq[:], ps("mq"), NO_TABLE)
+    st_q = merge_a(T.px[:, HP:CA], T.xq[:], T.dq[:], T.tq[:], ps("mq"), NO_TABLE)
     (s_l1,) = merge_b(st_1, T.t1[:], ps("m1"), [ps("l1")])
     s_gq, s_gp = merge_b(st_q, T.tq[:], ps("mq"), [T.gq[:], ps("gp")])
     V.wait_ge(s_l1, 1)
@@ -116,10 +203,10 @@ def rank_program(g, core, T, topo):
     s_la, s_lp = merge_b(st_2, T.t2[:], ps("m2"), [T.la[:], ps("lp")])
 
     g.wait_ge(s_gq, 1)
-    send(nxt, T.gv[:], T.gq[:], sem.arr4, RING)
-    send(prv, T.gn[:], T.gq[:], sem.arr5, RING)
+    send(nxt, T.gv[:], T.gq[:], sem.arr4, e_nxt)
+    send(prv, T.gn[:], T.gq[:], sem.arr5, e_prv)
     g.wait_ge(s_la, 1)
-    send(partner, T.lb[:], T.la[:], sem.arr3, CABLE)
+    send(partner, T.lb[:], T.la[:], sem.arr3, e_par)
 
     s_sq, s_pp, s_wp = new(), new(), new()
     S.activation(T.d1[:], T.d1[:], F.Sigmoid).then_inc(s_pp, 1)
@@ -154,12 +241,15 @@ def rank_program(g, core, T, topo):
     V.tensor_tensor(T.yb[:, 0:HP], ps("wp"), T.d3[:], A.mult).then_inc(s_yp, 1)
     V.wait_ge(s_wq, 1)
     V.wait_ge(s_p5, 1)
-    V.tensor_tensor(T.yb[:, HP:C], ps("wq"), T.d5[:], A.mult).then_inc(s_yq, 1)
+    V.tensor_tensor(T.yb[:, HP:CA], ps("wq"), T.d5[:], A.mult).then_inc(s_yq, 1)
 
     Y.wait_ge(s_yp, 1)
     Y.dma_start(T.y[:, 0:HP], T.yb[:, 0:HP]).then_inc(sem.stored, 16)
     Y.wait_ge(s_yq, 1)
-    Y.dma_start(T.y[:, HP:C], T.yb[:, HP:C]).then_inc(sem.stored, 16)
+    Y.dma_start(T.y[:, HP:CA], T.yb[:, HP:CA]).then_inc(sem.stored, 16)
+    S.wait_ge(sem.arry, n_home)
+    S.dma_start(T.y[:, CA:C], T.yb[:, CA:C]).then_inc(sem.storedb, 16)
+    S.wait_ge(sem.storedb, 16)
     Y.wait_ge(sem.stored, 32)
 
     g.wait_ge(sem.sent, sent[0])

from concourse.mybir import AluOpType, ActivationFunctionType

WORLD = 512
C = 256
CB = 48
CA = C - CB
HP = 80
HQ = CA - HP

R_T0 = 5.69
R_SCALE = 0.15951068197070614
R_GAMMA = 0.007537815109826294
SQ_SCALE = 0.9778153589291791
SQ_BIAS = 0.45741611243474367
GAMMA = -0.20580551923485052

SCRATCH = {"xs": ("sbuf", [128, C], "float32"), "yb": ("sbuf", [128, C], "bfloat16"), "px": ("psum", [128, CA], "float32")}
for _n in ("xb", "xc", "lb", "la", "d1", "d2", "d3", "t1", "t2"):
    SCRATCH[_n] = ("sbuf", [128, HP], "float32")
for _n in ("xq", "gv", "gn", "gq", "dq", "d4", "d5", "tq", "t4"):
    SCRATCH[_n] = ("sbuf", [128, HQ], "float32")
for _n in ("xh", "hxq", "hgv", "hgn", "hgq", "hdq", "hd4", "hd5", "htq", "ht4"):
    SCRATCH[_n] = ("sbuf", [128, CB], "float32")
SCRATCH["yh"] = ("sbuf", [128, CB], "bfloat16")
PS_P = ("m1", "m2", "l1", "lp", "wp")
PS_Q = ("mq", "m4", "gp", "hp", "wq")
PS_W = max(HP, HQ)
for _k in range((len(PS_P + PS_Q) + 2) // 3):
    SCRATCH["ps%d" % _k] = ("psum", [128, 3 * PS_W], "float32")
PS_B = ("px", "mq", "m4", "gp", "hp", "wq")
SCRATCH["pb"] = ("psum", [128, len(PS_B) * CB], "float32")
N_CSEM = 45
SEMAPHORES = ["loaded", "loadb", "arr1", "arr2", "arrq", "arr3", "arr4", "arr5", "arrh", "arry", "sent", "stored",
              "storedb"] + ["c%d" % i for i in range(N_CSEM)]


def rank_program(g, core, T, topo):
    def same_chip(a, b):
        return topo.host(a) == topo.host(b) and topo.chip(a) == topo.chip(b)

    if not [c for c in T.cores if same_chip(c, core)]:
        return

    def helper_of(c):
        return [k for k in range(WORLD) if same_chip(k, c) and topo.die(k) != topo.die(c) and T.rank_of(k) is None
                and all(topo.may_write(k, d) for d in T.cores if d != c and topo.may_write(c, d))][0]

    helpers = [helper_of(c) for c in T.cores]
    if T.rank_of(core) is not None:
        lane, is_rank = list(T.cores), True
    elif core in helpers:
        lane, is_rank = helpers, False
    else:
        return

    V, S, Y = g.vector, g.scalar, g.sync
    A, F = AluOpType, ActivationFunctionType
    sem = T.sem

    my_rack = topo.rack(topo.host(core))
    ring = [c for c in lane if topo.rack(topo.host(c)) == my_rack]
    i = ring.index(core)
    nxt, prv = ring[(i + 1) % len(ring)], ring[(i - 1) % len(ring)]
    partner = [c for c in lane if topo.rack(topo.host(c)) != my_rack
               and topo.chip(c) == topo.chip(core) and topo.may_write(core, c)][0]

    def deal(src, dst, k):
        e = [j for j in range(16) if (topo.mask(src, dst) >> j) & 1]
        return e[k::2]

    used = [0]

    def new():
        used[0] += 1
        return sem["c%d" % (used[0] - 1)]

    sent = [0]

    def send(dst, out_ap, in_ap, rsem, e):
        rid, pid = topo.addr(dst, core)
        g.remote_dma(out_ap, in_ap, rsem, sem.sent, pid, rid, sum(1 << j for j in e))
        sent[0] += len(e)

    RING, CABLE = 0, 1

    NO_TABLE = (((F.Abs, {}), (F.Relu, {"scale": -1.0, "bias": R_T0}), (F.Square, {"scale": R_SCALE}), (F.Square, {})),
                R_GAMMA)
    WITH_TABLE = (((F.Abs, {}), (F.Sigmoid, {"scale": -1.0}), (F.Square, {"scale": SQ_SCALE, "bias": SQ_BIAS})), GAMMA)

    def merge_a(acc, other, d, t, m, way):
        s = new()
        V.tensor_tensor(d, acc, other, A.subtract).then_inc(s, 1)
        src = d
        for func, kw in way[0]:
            S.wait_ge(s, 1)
            s = new()
            S.activation(t, src, func, **kw).then_inc(s, 1)
            src = t
        s_m, s_mg = new(), new()
        V.tensor_tensor(m, acc, other, A.max).then_inc(s_m, 1)
        V.wait_ge(s_m, 1)
        V.tensor_scalar(m, m, way[1], None, A.add).then_inc(s_mg, 1)
        return s, s_mg

    def merge_b(st, t, m, outs):
        V.wait_ge(st[1], 1)
        V.wait_ge(st[0], 1)
        res = []
        for out in outs:
            res.append(new())
            V.tensor_tensor(out, m, t, A.add).then_inc(res[-1], 1)
        return res

    if not is_rank:
        rank = T.cores[helpers.index(core)]

        def pb(name):
            k = PS_B.index(name)
            return T.pb[:, k * CB:(k + 1) * CB]

        r_ring = [c for c in T.cores if topo.rack(topo.host(c)) == my_rack]
        n_in = len(deal(rank, r_ring[(r_ring.index(rank) + 1) % len(r_ring)], RING))
        e_nxt, e_prv, e_par = deal(core, nxt, RING), deal(core, prv, RING), deal(core, partner, RING)
        e_home = [j for j in e_nxt if (topo.mask(core, rank) >> j) & 1]
        n_prv, n_nxt, n_par = len(deal(prv, core, RING)), len(deal(nxt, core, RING)), len(deal(partner, core, RING))

        g.wait_ge(sem.arrh, n_in)
        send(partner, T.hxq[:], T.xh[:], sem.arrq, e_par)

        s_ap = new()
        V.wait_ge(sem.arrh, n_in)
        V.tensor_copy(pb("px"), T.xh[:]).then_inc(s_ap, 1)
        V.wait_ge(s_ap, 1)
        V.wait_ge(sem.arrq, n_par)
        st_q = merge_a(pb("px"), T.hxq[:], T.hdq[:], T.htq[:], pb("mq"), NO_TABLE)
        s_gq, s_gp = merge_b(st_q, T.htq[:], pb("mq"), [T.hgq[:], pb("gp")])

        g.wait_ge(s_gq, 1)
        send(nxt, T.hgv[:], T.hgq[:], sem.arr4, e_nxt)
        send(prv, T.hgn[:], T.hgq[:], sem.arr5, e_prv)

        s_sq = new()
        S.activation(T.hdq[:], T.hdq[:], F.Sigmoid).then_inc(s_sq, 1)
        V.wait_ge(s_gp, 1)
        V.wait_ge(sem.arr4, n_prv)
        st_4 = merge_a(pb("gp"), T.hgv[:], T.hd4[:], T.ht4[:], pb("m4"), WITH_TABLE)
        (s_hp,) = merge_b(st_4, T.ht4[:], pb("m4"), [pb("hp")])
        s_s4, s_wq, s_d5, s_p5, s_y = new(), new(), new(), new(), new()
        S.activation(T.hd4[:], T.hd4[:], F.Sigmoid).then_inc(s_s4, 1)
        V.wait_ge(s_sq, 1)
        V.wait_ge(s_s4, 1)
        V.tensor_tensor(pb("wq"), T.hdq[:], T.hd4[:], A.mult).then_inc(s_wq, 1)
        V.wait_ge(s_hp, 1)
        V.wait_ge(sem.arr5, n_nxt)
        V.tensor_tensor(T.hd5[:], pb("hp"), T.hgn[:], A.subtract).then_inc(s_d5, 1)
        S.wait_ge(s_d5, 1)
        S.activation(T.hd5[:], T.hd5[:], F.Sigmoid).then_inc(s_p5, 1)
        V.wait_ge(s_wq, 1)
        V.wait_ge(s_p5, 1)
        V.tensor_tensor(T.yh[:], pb("wq"), T.hd5[:], A.mult).then_inc(s_y, 1)

        g.wait_ge(s_y, 1)
        send(rank, T.yb[:, CA:C], T.yh[:], sem.arry, e_home)
        g.wait_ge(sem.sent, sent[0])
        return

    helper = helpers[T.rank_of(core)]

    def ps(name):
        k = (PS_P + PS_Q).index(name)
        w = HP if name in PS_P else HQ
        return T["ps%d" % (k // 3)][:, (k % 3) * PS_W:(k % 3) * PS_W + w]

    e_nxt, e_prv, e_par = deal(core, nxt, RING), deal(core, prv, RING), deal(core, partner, CABLE)
    e_help = [j for j in e_nxt if (topo.mask(core, helper) >> j) & 1]
    n_prv, n_nxt, n_par = len(deal(prv, core, RING)), len(deal(nxt, core, RING)), len(deal(partner, core, CABLE))
    h_ring = [c for c in helpers if topo.rack(topo.host(c)) == my_rack]
    n_home = len(deal(helper, h_ring[(h_ring.index(helper) + 1) % len(h_ring)], RING))

    S.dma_start(T.xs[:, CA:C], T.x[:, CA:C]).then_inc(sem.loadb, 16)
    Y.dma_start(T.xs[:, 0:CA], T.x[:, 0:CA]).then_inc(sem.loaded, 16)

    g.wait_ge(sem.loadb, 16)
    send(helper, T.xh[:], T.xs[:, CA:C], sem.arrh, e_help)
    g.wait_ge(sem.loaded, 16)
    send(nxt, T.xb[:], T.xs[:, 0:HP], sem.arr1, e_nxt)
    send(partner, T.xq[:], T.xs[:, HP:CA], sem.arrq, e_par)
    send(prv, T.xc[:], T.xs[:, 0:HP], sem.arr2, e_prv)

    s_ap = new()
    V.wait_ge(sem.loaded, 16)
    V.tensor_copy(T.px[:], T.xs[:, 0:CA]).then_inc(s_ap, 1)
    V.wait_ge(s_ap, 1)
    V.wait_ge(sem.arr1, n_prv)
    st_1 = merge_a(T.px[:, 0:HP], T.xb[:], T.d1[:], T.t1[:], ps("m1"), NO_TABLE)
    V.wait_ge(sem.arrq, n_par)
    st_q = merge_a(T.px[:, HP:CA], T.xq[:], T.dq[:], T.tq[:], ps("mq"), NO_TABLE)
    (s_l1,) = merge_b(st_1, T.t1[:], ps("m1"), [ps("l1")])
    s_gq, s_gp = merge_b(st_q, T.tq[:], ps("mq"), [T.gq[:], ps("gp")])
    V.wait_ge(s_l1, 1)
    V.wait_ge(sem.arr2, n_nxt)
    st_2 = merge_a(ps("l1"), T.xc[:], T.d2[:], T.t2[:], ps("m2"), NO_TABLE)
    s_la, s_lp = merge_b(st_2, T.t2[:], ps("m2"), [T.la[:], ps("lp")])

    g.wait_ge(s_gq, 1)
    send(nxt, T.gv[:], T.gq[:], sem.arr4, e_nxt)
    send(prv, T.gn[:], T.gq[:], sem.arr5, e_prv)
    g.wait_ge(s_la, 1)
    send(partner, T.lb[:], T.la[:], sem.arr3, e_par)

    s_sq, s_pp, s_wp = new(), new(), new()
    S.activation(T.d1[:], T.d1[:], F.Sigmoid).then_inc(s_pp, 1)
    S.activation(T.d2[:], T.d2[:], F.Sigmoid).then_inc(s_pp, 1)
    S.activation(T.dq[:], T.dq[:], F.Sigmoid).then_inc(s_sq, 1)
    V.wait_ge(s_pp, 2)
    V.tensor_tensor(ps("wp"), T.d1[:], T.d2[:], A.mult).then_inc(s_wp, 1)

    V.wait_ge(s_gp, 1)
    V.wait_ge(sem.arr4, n_prv)
    st_4 = merge_a(ps("gp"), T.gv[:], T.d4[:], T.t4[:], ps("m4"), WITH_TABLE)
    (s_hp,) = merge_b(st_4, T.t4[:], ps("m4"), [ps("hp")])
    s_s4, s_wq = new(), new()
    S.activation(T.d4[:], T.d4[:], F.Sigmoid).then_inc(s_s4, 1)
    V.wait_ge(s_sq, 1)
    V.wait_ge(s_s4, 1)
    V.tensor_tensor(ps("wq"), T.dq[:], T.d4[:], A.mult).then_inc(s_wq, 1)

    s_d3, s_d5, s_p3, s_p5, s_yp, s_yq = new(), new(), new(), new(), new(), new()
    V.wait_ge(s_lp, 1)
    V.wait_ge(sem.arr3, n_par)
    V.tensor_tensor(T.d3[:], ps("lp"), T.lb[:], A.subtract).then_inc(s_d3, 1)
    V.wait_ge(s_hp, 1)
    V.wait_ge(sem.arr5, n_nxt)
    V.tensor_tensor(T.d5[:], ps("hp"), T.gn[:], A.subtract).then_inc(s_d5, 1)
    S.wait_ge(s_d3, 1)
    S.activation(T.d3[:], T.d3[:], F.Sigmoid).then_inc(s_p3, 1)
    S.wait_ge(s_d5, 1)
    S.activation(T.d5[:], T.d5[:], F.Sigmoid).then_inc(s_p5, 1)
    V.wait_ge(s_wp, 1)
    V.wait_ge(s_p3, 1)
    V.tensor_tensor(T.yb[:, 0:HP], ps("wp"), T.d3[:], A.mult).then_inc(s_yp, 1)
    V.wait_ge(s_wq, 1)
    V.wait_ge(s_p5, 1)
    V.tensor_tensor(T.yb[:, HP:CA], ps("wq"), T.d5[:], A.mult).then_inc(s_yq, 1)

    Y.wait_ge(s_yp, 1)
    Y.dma_start(T.y[:, 0:HP], T.yb[:, 0:HP]).then_inc(sem.stored, 16)
    Y.wait_ge(s_yq, 1)
    Y.dma_start(T.y[:, HP:CA], T.yb[:, HP:CA]).then_inc(sem.stored, 16)
    S.wait_ge(sem.arry, n_home)
    S.dma_start(T.y[:, CA:C], T.yb[:, CA:C]).then_inc(sem.storedb, 16)
    S.wait_ge(sem.storedb, 16)
    Y.wait_ge(sem.stored, 32)

    g.wait_ge(sem.sent, sent[0])
